import numpy as np
import ml_dtypes


def mxq(x, axis, fmt="e4m3"):
    dtype, down = {"e4m3": (ml_dtypes.float8_e4m3fn, 7), "e5m2": (ml_dtypes.float8_e5m2, 14)}[fmt]
    v = np.moveaxis(np.asarray(x, np.float32).astype(ml_dtypes.bfloat16).astype(np.float64), axis, -1)
    blocks = v.reshape(v.shape[:-1] + (-1, 32))
    amax = np.abs(blocks).max(-1, keepdims=True)
    byte = np.maximum(np.where(amax > 0, np.frexp(amax)[1] - 1 + 127, 0) - down, 1)
    scale = np.exp2(byte - 127.0)
    codes = (blocks / scale).astype(np.float32).astype(dtype).astype(np.float64)
    return np.moveaxis((codes * scale).reshape(v.shape), -1, axis)


WIDE = False


def mx_kscale(k):
    if not WIDE:
        return np.ones(k)
    levels = np.array([30, -30])
    if k % 512:
        return np.exp2(np.random.permutation(np.resize(levels, k // 32))).repeat(32)
    a = np.empty((k // 512, 16))
    for p in range(k // 512):
        a[p, :8] = np.random.permutation(np.resize(levels, 8))
        for g in range(8):
            far = levels[np.abs(levels - a[p, g]) >= 10]
            a[p, g + 8] = far[np.random.randint(len(far))]
    return np.exp2(a.ravel()).repeat(32)


def f64(x):
    return np.asarray(x).astype(np.float64)


E2M1 = np.array([0.0, 0.5, 1.0, 1.5, 2.0, 3.0, 4.0, 6.0, -0.0, -0.5, -1.0, -1.5, -2.0, -3.0, -4.0, -6.0])


def pack_weight(w, fmt):
    k, n = w.shape
    w = f64(np.asarray(w, np.float32).astype(ml_dtypes.bfloat16)).reshape(k // 32, 32, n)
    amax = np.abs(w).max(1)
    if fmt == "e4m3":
        byte = np.frexp(amax)[1] - 1 + 127 - 7
    else:
        mant, ex = np.frexp(amax / 6.0)
        byte = np.where(mant > 0.5, ex, ex - 1) + 127
    byte = np.clip(np.where(amax > 0, byte, 1), 1, 254)
    scaled = (w * np.exp2(127.0 - byte)[:, None, :]).reshape(k, n).astype(np.float32)
    by_word = np.ascontiguousarray(scaled.reshape(k // 512, 128, 4, n).transpose(0, 1, 3, 2))
    if fmt == "e4m3":
        words = by_word.astype(ml_dtypes.float8_e4m3fn).view(np.uint8)
    else:
        c = by_word.astype(ml_dtypes.float4_e2m1fn).view(np.uint8) & 0xF
        words = (c[..., 0::2] | (c[..., 1::2] << 4)).reshape(k // 512, 128, 2 * n)
    return np.ascontiguousarray(words), np.ascontiguousarray(byte.astype(np.uint8).reshape(k // 512, 16, n))


def unpack_weight(words, scales, fmt):
    g, _, n = scales.shape
    words = np.ascontiguousarray(words).reshape(g, 128, n, -1)
    if fmt == "e4m3":
        vals = words.view(ml_dtypes.float8_e4m3fn).astype(np.float64)
    else:
        nib = np.empty((g, 128, n, 4), np.uint8)
        nib[..., 0::2] = words & 0xF
        nib[..., 1::2] = words >> 4
        vals = E2M1[nib]
    vals = vals * np.repeat(np.exp2(scales.astype(np.float64) - 127.0), 8, axis=1)[..., None]
    return vals.transpose(0, 1, 3, 2).reshape(g * 512, n)


K, T, N = 1024, 512, 512


def setup_inputs():
    n = np.random.standard_normal
    fk = mx_kscale(K)
    wap = pack_weight(n((K, N)) * 1 / np.sqrt(K) * fk[:, None], "e2m1")
    wbp = pack_weight(n((K, N)) * 1 / np.sqrt(K) * fk[:, None], "e4m3")
    return {
        "xf": (n((K, T)) * 1.2).astype(np.float32),
        "lo": (np.random.uniform(-1.0, -0.4, (K, 1))).astype(np.float32),
        "hi": (np.random.uniform(0.4, 1.0, (K, 1))).astype(np.float32),
        "fa": (np.random.uniform(0.5, 2.0, (K, 1)) / fk[:, None]).astype(np.float32),
        "fb": (np.random.uniform(0.5, 2.0, (K, 1)) / fk[:, None]).astype(np.float32),
        "wa_words": wap[0],
        "wa_scales": wap[1],
        "wb_words": wbp[0],
        "wb_scales": wbp[1],
    }


def reference(xf, lo, hi, fa, fb, wa_words, wa_scales, wb_words, wb_scales):
    wau = unpack_weight(wa_words, wa_scales, "e2m1")
    wbu = unpack_weight(wb_words, wb_scales, "e4m3")
    b = np.maximum(np.minimum(f64(xf), f64(hi)), f64(lo))
    xa = b * f64(fa)
    xc = (f64(xf) - b) * f64(fb)
    xaq = mxq(xa, 0, "e4m3")
    xcq = mxq(xc, 0, "e5m2")
    y = wau.T @ xaq + wbu.T @ xcq
    return y

@@ -1,0 +1,171 @@
+from contextlib import ExitStack
+
+import concourse.mybir as mybir
+
+K, T, N = 1024, 512, 512
+FLOPS = 2 * 2 * K * T * N
+
+F32 = mybir.dt.float32
+BF16 = mybir.dt.bfloat16
+I32 = mybir.dt.int32
+U32 = mybir.dt.uint32
+U8 = mybir.dt.uint8
+E4M3X4 = mybir.dt.float8_e4m3fn_x4
+E5M2X4 = mybir.dt.float8_e5m2_x4
+E2M1X4 = mybir.dt.float4_e2m1fn_x4
+ALU = mybir.AluOpType
+ACT = mybir.ActivationFunctionType
+
+P = 128
+PACK = 4
+PASSES = K // (P * PACK)
+N_TILES = N // P
+QUARTER = T // 4
+RUN = 4
+
+
+def tile_mix_kept_and_cut_off_kernel(tc, xf, lo, hi, fa, fb, wa_words, wa_scales, wb_words, wb_scales, out):
+    nc = tc.nc
+    with ExitStack() as ctx:
+        sb = ctx.enter_context(tc.tile_pool(name="sb", bufs=1))
+        ps = ctx.enter_context(tc.psum_pool(name="ps", bufs=1))
+        ctx.enter_context(tc.manual_schedule())
+
+        def tiles(name, shape, dtype, count):
+            return [sb.tile(shape, dtype, name="%s%d" % (name, i), align_bytes=64) for i in range(count)]
+
+        x_rows = xf.rearrange("(g p j) t -> g j p t", g=PASSES, j=PACK)
+        x = [tiles("x%d_" % g, [P, T], F32, PACK) for g in range(PASSES)]
+        kept = [tiles("kept%d_" % g, [P, T], F32, PACK) for g in range(PASSES)]
+        cut = [tiles("cut%d_" % g, [P, T], F32, PACK) for g in range(PASSES)]
+        xa_rows = tiles("xa_rows", [P, PACK, T], BF16, PASSES)
+        xc_rows = tiles("xc_rows", [P, PACK, T], BF16, PASSES)
+        xa_packed = tiles("xa_packed", [P, T, PACK], BF16, PASSES)
+        xc_packed = tiles("xc_packed", [P, T, PACK], BF16, PASSES)
+        xa_codes = tiles("xa_codes", [P, T], U32, PASSES)
+        xc_codes = tiles("xc_codes", [P, T], U32, PASSES)
+        xa_exp = tiles("xa_exp", [P, T], U8, PASSES)
+        xc_exp = tiles("xc_exp", [P, T], U8, PASSES)
+        lo_sb, hi_sb, fa_sb, fb_sb = tiles("per_k", [P, PASSES, 2 * PACK], F32, 4)
+        wa = sb.tile([P, PASSES, 2 * N], U8, name="wa", align_bytes=64)
+        wb = sb.tile([P, PASSES, 4 * N], U8, name="wb", align_bytes=64)
+        wa_exp, wb_exp = tiles("w_exp", [P, PASSES, N], U8, 2)
+        result = tiles("result", [P, T], F32, N_TILES)
+        warm = sb.tile([P, 8], F32, name="warm")
+        acc = [ps.tile([P, T], F32, name="acc%d" % n) for n in range(N_TILES)]
+
+        halves = [slice(0, T // 2), slice(T // 2, T)]
+        for vec, dst in ((hi, hi_sb), (lo, lo_sb), (fa, fa_sb), (fb, fb_sb)):
+            nc.scalar.dma_start(out=dst[:, :, 0:PACK], in_=vec.rearrange("(g p j) o -> p g (j o)", g=PASSES, j=PACK))
+        nc.vector.memset(warm[:, 0:1], 0.0)
+        for plane in (wb_exp, wa_exp):
+            nc.vector.memset(plane[:].bitcast(I32), 0)
+        nc.scalar.activation(out=warm[:, 1:2], in_=warm[:, 0:1], func=ACT.Copy)
+        for g in range(PASSES):
+            for j in range(PACK):
+                for cols in (halves if g == 0 and j == 0 else [slice(0, T)]):
+                    nc.sync.dma_start(out=x[g][j][:, cols], in_=x_rows[g, j][:, cols])
+        nc.sync.dma_start(out=wb[:].bitcast(I32), in_=wb_words.rearrange("z p n r -> p z (n r)").bitcast(I32))
+        for q in range(4):
+            nc.sync.dma_start(out=wb_exp[32 * q : 32 * q + 4, :, :].bitcast(I32),
+                              in_=wb_scales[:, 4 * q : 4 * q + 4, :].rearrange("z r n -> r z n").bitcast(I32))
+        for q in range(4):
+            nc.sync.dma_start(out=wa_exp[32 * q : 32 * q + 4, :, :].bitcast(I32),
+                              in_=wa_scales[:, 4 * q : 4 * q + 4, :].rearrange("z r n -> r z n").bitcast(I32))
+        nc.sync.dma_start(out=wa[:].bitcast(I32), in_=wa_words.rearrange("z p b -> p z b").bitcast(I32))
+
+        def clamp(g, j, cols=slice(0, T)):
+            nc.vector.tensor_scalar(out=kept[g][j][:, cols], in0=x[g][j][:, cols], scalar1=hi_sb[:, g, j : j + 1],
+                                    scalar2=lo_sb[:, g, j : j + 1], op0=ALU.min, op1=ALU.max)
+
+        def subtract(g, j, cols=slice(0, T)):
+            nc.vector.tensor_tensor(out=cut[g][j][:, cols], in0=x[g][j][:, cols], in1=kept[g][j][:, cols], op=ALU.subtract)
+
+        def scale_xa(g, j):
+            nc.scalar.activation(out=xa_rows[g][:, j, :], in_=kept[g][j][:], func=ACT.Copy, scale=fa_sb[:, g, j : j + 1])
+
+        def scale_xa_vector(g, j):
+            nc.vector.tensor_scalar(out=xa_rows[g][:, j, :], in0=kept[g][j][:], scalar1=fa_sb[:, g, j : j + 1],
+                                    scalar2=None, op0=ALU.mult)
+
+        def scale_xc(g, j):
+            nc.scalar.activation(out=xc_rows[g][:, j, :], in_=cut[g][j][:], func=ACT.Copy, scale=fb_sb[:, g, j : j + 1])
+
+        def scale_xc_vector(g, j):
+            nc.vector.tensor_scalar(out=xc_rows[g][:, j, :], in0=cut[g][j][:], scalar1=fb_sb[:, g, j : j + 1],
+                                    scalar2=None, op0=ALU.mult)
+
+        def pack(copy, packed, rows, t0, t1):
+            copy(out=packed[:, t0:t1, :].rearrange("p (c i) j -> p c j i", i=RUN),
+                 in_=rows[:, :, t0:t1].rearrange("p j (c i) -> p c j i", i=RUN))
+
+        def quantize(packed, codes, exps, fmt, t0, t1):
+            nc.vector.quantize_mx(out=codes[:, t0:t1].bitcast(fmt), scales=exps[:, t0:t1],
+                                  in_=packed[:, t0:t1, :].rearrange("p t j -> p (t j)"))
+
+        def multiply_xc(g):
+            for n in range(N_TILES):
+                nc.tensor.matmul_mx(out=acc[n][:], lhsT=wb[:, g, 4 * P * n : 4 * P * (n + 1)].bitcast(E4M3X4),
+                                    lhsT_scale=wb_exp[:, g, P * n : P * (n + 1)],
+                                    rhs=xc_codes[g][:].bitcast(E5M2X4), rhs_scale=xc_exp[g][:],
+                                    start=(g == 0), stop=False)
+
+        def multiply_xa(g, t0, t1, last):
+            for n in range(N_TILES):
+                nc.tensor.matmul_mx(out=acc[n][:, t0:t1], lhsT=wa[:, g, 2 * P * n : 2 * P * (n + 1)].bitcast(E2M1X4),
+                                    lhsT_scale=wa_exp[:, g, P * n : P * (n + 1)],
+                                    rhs=xa_codes[g][:, t0:t1].bitcast(E4M3X4), rhs_scale=xa_exp[g][:, t0:t1],
+                                    start=False, stop=last)
+
+        on_vector = nc.vector.tensor_copy
+        on_scalar = nc.scalar.copy
+
+        for half in halves:
+            clamp(0, 0, half)
+        scale_xa(0, 0)
+        for half in halves:
+            subtract(0, 0, half)
+        scale_xc(0, 0)
+        clamp(0, 1)
+        for j in range(1, PACK - 1):
+            clamp(0, j + 1)
+            scale_xa(0, j)
+            subtract(0, j)
+            scale_xc(0, j)
+        clamp(1, 0)
+        subtract(0, 3)
+        scale_xc(0, 3)
+        scale_xa(0, 3)
+        for j in range(2):
+            clamp(1, j + 1)
+            subtract(1, j)
+            scale_xc(1, j)
+        pack(on_vector, xc_packed[0], xc_rows[0], 0, T)
+        clamp(1, 3)
+        quantize(xc_packed[0], xc_codes[0], xc_exp[0], E5M2X4, 0, T)
+        multiply_xc(0)
+        pack(on_scalar, xa_packed[0], xa_rows[0], 0, T)
+        subtract(1, 2)
+        scale_xc(1, 2)
+        subtract(1, 3)
+        scale_xa(1, 0)
+        quantize(xa_packed[0], xa_codes[0], xa_exp[0], E4M3X4, 0, T)
+        multiply_xa(0, 0, T, False)
+        scale_xc_vector(1, 3)
+        scale_xa_vector(1, 3)
+        pack(on_vector, xc_packed[1], xc_rows[1], 0, T)
+        scale_xa(1, 1)
+        scale_xa(1, 2)
+        pack(on_scalar, xa_packed[1], xa_rows[1], 2 * QUARTER, T)
+        pack(on_vector, xa_packed[1], xa_rows[1], 0, QUARTER)
+        quantize(xc_packed[1], xc_codes[1], xc_exp[1], E5M2X4, 0, T)
+        multiply_xc(1)
+        pack(on_vector, xa_packed[1], xa_rows[1], QUARTER, 2 * QUARTER)
+        quantize(xa_packed[1], xa_codes[1], xa_exp[1], E4M3X4, 2 * QUARTER, T)
+        quantize(xa_packed[1], xa_codes[1], xa_exp[1], E4M3X4, 0, 2 * QUARTER)
+        multiply_xa(1, 0, T, True)
+        for n in range(N_TILES):
+            copy = on_scalar if n % 2 == 0 else on_vector
+            for cols in (halves if n == 0 else [slice(0, T)]):
+                copy(out=result[n][:, cols], in_=acc[n][:, cols])
+                nc.sync.dma_start(out=out[P * n : P * (n + 1), cols], in_=result[n][:, cols])

@@ -46,7 +46,7 @@ def tile_mix_kept_and_cut_off_kernel(tc, xf, lo, hi, fa, fb, wa_words, wa_scales
         xc_codes = tiles("xc_codes", [P, T], U32, PASSES)
         xa_exp = tiles("xa_exp", [P, T], U8, PASSES)
         xc_exp = tiles("xc_exp", [P, T], U8, PASSES)
-        lo_sb, hi_sb, fa_sb, fb_sb = tiles("per_k", [P, PASSES, 2 * PACK], F32, 4)
+        lo_sb, hi_sb, fa_sb, fb_sb = [tiles(name, [P, PACK], F32, PASSES) for name in ("lo", "hi", "fa", "fb")]
         wa = sb.tile([P, PASSES, 2 * N], U8, name="wa", align_bytes=64)
         wb = sb.tile([P, PASSES, 4 * N], U8, name="wb", align_bytes=64)
         wa_exp, wb_exp = tiles("w_exp", [P, PASSES, N], U8, 2)
@@ -55,16 +55,31 @@ def tile_mix_kept_and_cut_off_kernel(tc, xf, lo, hi, fa, fb, wa_words, wa_scales
         acc = [ps.tile([P, T], F32, name="acc%d" % n) for n in range(N_TILES)]
 
         halves = [slice(0, T // 2), slice(T // 2, T)]
-        for vec, dst in ((hi, hi_sb), (lo, lo_sb), (fa, fa_sb), (fb, fb_sb)):
-            nc.scalar.dma_start(out=dst[:, :, 0:PACK], in_=vec.rearrange("(g p j) o -> p g (j o)", g=PASSES, j=PACK))
+        def load_per_k(queue, vec, dst, g):
+            queue.dma_start(out=dst[g][:, 0:PACK], in_=vec.rearrange("(g p j) o -> g p (j o)", g=PASSES, j=PACK)[g])
+
+        def load_x(g, j, cols=slice(0, T)):
+            nc.sync.dma_start(out=x[g][j][:, cols], in_=x_rows[g, j][:, cols])
+
+        load_per_k(nc.sync, hi, hi_sb, 0)
+        load_per_k(nc.sync, lo, lo_sb, 0)
+        for half in halves:
+            load_x(0, 0, half)
+        load_per_k(nc.scalar, fa, fa_sb, 0)
+        load_per_k(nc.scalar, fb, fb_sb, 0)
         nc.vector.memset(warm[:, 0:1], 0.0)
         for plane in (wb_exp, wa_exp):
             nc.vector.memset(plane[:].bitcast(I32), 0)
         nc.scalar.activation(out=warm[:, 1:2], in_=warm[:, 0:1], func=ACT.Copy)
-        for g in range(PASSES):
-            for j in range(PACK):
-                for cols in (halves if g == 0 and j == 0 else [slice(0, T)]):
-                    nc.sync.dma_start(out=x[g][j][:, cols], in_=x_rows[g, j][:, cols])
+        for j in range(1, PACK):
+            load_x(0, j)
+        load_per_k(nc.sync, hi, hi_sb, 1)
+        load_per_k(nc.sync, lo, lo_sb, 1)
+        load_x(1, 0)
+        load_per_k(nc.sync, fb, fb_sb, 1)
+        load_per_k(nc.sync, fa, fa_sb, 1)
+        for j in range(1, PACK):
+            load_x(1, j)
         nc.sync.dma_start(out=wb[:].bitcast(I32), in_=wb_words.rearrange("z p n r -> p z (n r)").bitcast(I32))
         for q in range(4):
             nc.sync.dma_start(out=wb_exp[32 * q : 32 * q + 4, :, :].bitcast(I32),
@@ -75,24 +90,24 @@ def tile_mix_kept_and_cut_off_kernel(tc, xf, lo, hi, fa, fb, wa_words, wa_scales
         nc.sync.dma_start(out=wa[:].bitcast(I32), in_=wa_words.rearrange("z p b -> p z b").bitcast(I32))
 
         def clamp(g, j, cols=slice(0, T)):
-            nc.vector.tensor_scalar(out=kept[g][j][:, cols], in0=x[g][j][:, cols], scalar1=hi_sb[:, g, j : j + 1],
-                                    scalar2=lo_sb[:, g, j : j + 1], op0=ALU.min, op1=ALU.max)
+            nc.vector.tensor_scalar(out=kept[g][j][:, cols], in0=x[g][j][:, cols], scalar1=hi_sb[g][:, j : j + 1],
+                                    scalar2=lo_sb[g][:, j : j + 1], op0=ALU.min, op1=ALU.max)
 
         def subtract(g, j, cols=slice(0, T)):
             nc.vector.tensor_tensor(out=cut[g][j][:, cols], in0=x[g][j][:, cols], in1=kept[g][j][:, cols], op=ALU.subtract)
 
         def scale_xa(g, j):
-            nc.scalar.activation(out=xa_rows[g][:, j, :], in_=kept[g][j][:], func=ACT.Copy, scale=fa_sb[:, g, j : j + 1])
+            nc.scalar.activation(out=xa_rows[g][:, j, :], in_=kept[g][j][:], func=ACT.Copy, scale=fa_sb[g][:, j : j + 1])
 
         def scale_xa_vector(g, j):
-            nc.vector.tensor_scalar(out=xa_rows[g][:, j, :], in0=kept[g][j][:], scalar1=fa_sb[:, g, j : j + 1],
+            nc.vector.tensor_scalar(out=xa_rows[g][:, j, :], in0=kept[g][j][:], scalar1=fa_sb[g][:, j : j + 1],
                                     scalar2=None, op0=ALU.mult)
 
         def scale_xc(g, j):
-            nc.scalar.activation(out=xc_rows[g][:, j, :], in_=cut[g][j][:], func=ACT.Copy, scale=fb_sb[:, g, j : j + 1])
+            nc.scalar.activation(out=xc_rows[g][:, j, :], in_=cut[g][j][:], func=ACT.Copy, scale=fb_sb[g][:, j : j + 1])
 
         def scale_xc_vector(g, j):
-            nc.vector.tensor_scalar(out=xc_rows[g][:, j, :], in0=cut[g][j][:], scalar1=fb_sb[:, g, j : j + 1],
+            nc.vector.tensor_scalar(out=xc_rows[g][:, j, :], in0=cut[g][j][:], scalar1=fb_sb[g][:, j : j + 1],
                                     scalar2=None, op0=ALU.mult)
 
         def pack(copy, packed, rows, t0, t1):

@@ -20,7 +20,7 @@ P = 128
 PACK = 4
 PASSES = K // (P * PACK)
 N_TILES = N // P
-QUARTER = T // 4
+SPLIT = 192
 RUN = 4
 
 
@@ -61,7 +61,7 @@ def tile_mix_kept_and_cut_off_kernel(tc, xf, lo, hi, fa, fb, wa_words, wa_scales
         def load_x(g, j, cols=slice(0, T)):
             nc.sync.dma_start(out=x[g][j][:, cols], in_=x_rows[g, j][:, cols])
 
-        load_per_k(nc.sync, hi, hi_sb, 0)
+        load_per_k(nc.scalar, hi, hi_sb, 0)
         load_per_k(nc.sync, lo, lo_sb, 0)
         for half in halves:
             load_x(0, 0, half)
@@ -147,14 +147,15 @@ def tile_mix_kept_and_cut_off_kernel(tc, xf, lo, hi, fa, fb, wa_words, wa_scales
             scale_xa(0, j)
             subtract(0, j)
             scale_xc(0, j)
-        clamp(1, 0)
         subtract(0, 3)
         scale_xc(0, 3)
         scale_xa(0, 3)
-        for j in range(2):
-            clamp(1, j + 1)
+        for j in (0, 1):
+            clamp(1, j)
+        for j in (0, 1):
             subtract(1, j)
             scale_xc(1, j)
+        clamp(1, 2)
         pack(on_vector, xc_packed[0], xc_rows[0], 0, T)
         clamp(1, 3)
         quantize(xc_packed[0], xc_codes[0], xc_exp[0], E5M2X4, 0, T)
@@ -168,16 +169,18 @@ def tile_mix_kept_and_cut_off_kernel(tc, xf, lo, hi, fa, fb, wa_words, wa_scales
         multiply_xa(0, 0, T, False)
         scale_xc_vector(1, 3)
         scale_xa_vector(1, 3)
-        pack(on_vector, xc_packed[1], xc_rows[1], 0, T)
         scale_xa(1, 1)
         scale_xa(1, 2)
-        pack(on_scalar, xa_packed[1], xa_rows[1], 2 * QUARTER, T)
-        pack(on_vector, xa_packed[1], xa_rows[1], 0, QUARTER)
-        quantize(xc_packed[1], xc_codes[1], xc_exp[1], E5M2X4, 0, T)
+        for t0 in (0, T // 2):
+            pack(on_vector, xc_packed[1], xc_rows[1], t0, t0 + T // 2)
+        for t0 in (0, T // 2):
+            quantize(xc_packed[1], xc_codes[1], xc_exp[1], E5M2X4, t0, t0 + T // 2)
         multiply_xc(1)
-        pack(on_vector, xa_packed[1], xa_rows[1], QUARTER, 2 * QUARTER)
-        quantize(xa_packed[1], xa_codes[1], xa_exp[1], E4M3X4, 2 * QUARTER, T)
-        quantize(xa_packed[1], xa_codes[1], xa_exp[1], E4M3X4, 0, 2 * QUARTER)
+        pack(on_scalar, xa_packed[1], xa_rows[1], T // 2, T)
+        pack(on_scalar, xa_packed[1], xa_rows[1], SPLIT, T // 2)
+        pack(on_vector, xa_packed[1], xa_rows[1], 0, SPLIT)
+        for t0 in (T // 2, 0):
+            quantize(xa_packed[1], xa_codes[1], xa_exp[1], E4M3X4, t0, t0 + T // 2)
         multiply_xa(1, 0, T, True)
         for n in range(N_TILES):
             copy = on_scalar if n % 2 == 0 else on_vector

from contextlib import ExitStack

import concourse.mybir as mybir

K, T, N = 1024, 512, 512
FLOPS = 2 * 2 * K * T * N

F32 = mybir.dt.float32
BF16 = mybir.dt.bfloat16
I32 = mybir.dt.int32
U32 = mybir.dt.uint32
U8 = mybir.dt.uint8
E4M3X4 = mybir.dt.float8_e4m3fn_x4
E5M2X4 = mybir.dt.float8_e5m2_x4
E2M1X4 = mybir.dt.float4_e2m1fn_x4
ALU = mybir.AluOpType
ACT = mybir.ActivationFunctionType

P = 128
PACK = 4
PASSES = K // (P * PACK)
N_TILES = N // P
SPLIT = 192
RUN = 4


def tile_mix_kept_and_cut_off_kernel(tc, xf, lo, hi, fa, fb, wa_words, wa_scales, wb_words, wb_scales, out):
    nc = tc.nc
    with ExitStack() as ctx:
        sb = ctx.enter_context(tc.tile_pool(name="sb", bufs=1))
        ps = ctx.enter_context(tc.psum_pool(name="ps", bufs=1))
        ctx.enter_context(tc.manual_schedule())

        def tiles(name, shape, dtype, count):
            return [sb.tile(shape, dtype, name="%s%d" % (name, i), align_bytes=64) for i in range(count)]

        x_rows = xf.rearrange("(g p j) t -> g j p t", g=PASSES, j=PACK)
        x = [tiles("x%d_" % g, [P, T], F32, PACK) for g in range(PASSES)]
        kept = [tiles("kept%d_" % g, [P, T], F32, PACK) for g in range(PASSES)]
        cut = [tiles("cut%d_" % g, [P, T], F32, PACK) for g in range(PASSES)]
        xa_rows = tiles("xa_rows", [P, PACK, T], BF16, PASSES)
        xc_rows = tiles("xc_rows", [P, PACK, T], BF16, PASSES)
        xa_packed = tiles("xa_packed", [P, T, PACK], BF16, PASSES)
        xc_packed = tiles("xc_packed", [P, T, PACK], BF16, PASSES)
        xa_codes = tiles("xa_codes", [P, T], U32, PASSES)
        xc_codes = tiles("xc_codes", [P, T], U32, PASSES)
        xa_exp = tiles("xa_exp", [P, T], U8, PASSES)
        xc_exp = tiles("xc_exp", [P, T], U8, PASSES)
        lo_sb, hi_sb, fa_sb, fb_sb = [tiles(name, [P, PACK], F32, PASSES) for name in ("lo", "hi", "fa", "fb")]
        wa = sb.tile([P, PASSES, 2 * N], U8, name="wa", align_bytes=64)
        wb = sb.tile([P, PASSES, 4 * N], U8, name="wb", align_bytes=64)
        wa_exp, wb_exp = tiles("w_exp", [P, PASSES, N], U8, 2)
        result = tiles("result", [P, T], F32, N_TILES)
        warm = sb.tile([P, 8], F32, name="warm")
        acc = [ps.tile([P, T], F32, name="acc%d" % n) for n in range(N_TILES)]

        halves = [slice(0, T // 2), slice(T // 2, T)]
        def load_per_k(queue, vec, dst, g):
            queue.dma_start(out=dst[g][:, 0:PACK], in_=vec.rearrange("(g p j) o -> g p (j o)", g=PASSES, j=PACK)[g])

        def load_x(g, j, cols=slice(0, T)):
            nc.sync.dma_start(out=x[g][j][:, cols], in_=x_rows[g, j][:, cols])

        load_per_k(nc.scalar, hi, hi_sb, 0)
        load_per_k(nc.sync, lo, lo_sb, 0)
        for half in halves:
            load_x(0, 0, half)
        load_per_k(nc.scalar, fa, fa_sb, 0)
        load_per_k(nc.scalar, fb, fb_sb, 0)
        nc.vector.memset(warm[:, 0:1], 0.0)
        for plane in (wb_exp, wa_exp):
            nc.vector.memset(plane[:].bitcast(I32), 0)
        nc.scalar.activation(out=warm[:, 1:2], in_=warm[:, 0:1], func=ACT.Copy)
        for j in range(1, PACK):
            load_x(0, j)
        load_per_k(nc.sync, hi, hi_sb, 1)
        load_per_k(nc.sync, lo, lo_sb, 1)
        load_x(1, 0)
        load_per_k(nc.sync, fb, fb_sb, 1)
        load_per_k(nc.sync, fa, fa_sb, 1)
        for j in range(1, PACK):
            load_x(1, j)
        nc.sync.dma_start(out=wb[:].bitcast(I32), in_=wb_words.rearrange("z p n r -> p z (n r)").bitcast(I32))
        for q in range(4):
            nc.sync.dma_start(out=wb_exp[32 * q : 32 * q + 4, :, :].bitcast(I32),
                              in_=wb_scales[:, 4 * q : 4 * q + 4, :].rearrange("z r n -> r z n").bitcast(I32))
        for q in range(4):
            nc.sync.dma_start(out=wa_exp[32 * q : 32 * q + 4, :, :].bitcast(I32),
                              in_=wa_scales[:, 4 * q : 4 * q + 4, :].rearrange("z r n -> r z n").bitcast(I32))
        nc.sync.dma_start(out=wa[:].bitcast(I32), in_=wa_words.rearrange("z p b -> p z b").bitcast(I32))

        def clamp(g, j, cols=slice(0, T)):
            nc.vector.tensor_scalar(out=kept[g][j][:, cols], in0=x[g][j][:, cols], scalar1=hi_sb[g][:, j : j + 1],
                                    scalar2=lo_sb[g][:, j : j + 1], op0=ALU.min, op1=ALU.max)

        def subtract(g, j, cols=slice(0, T)):
            nc.vector.tensor_tensor(out=cut[g][j][:, cols], in0=x[g][j][:, cols], in1=kept[g][j][:, cols], op=ALU.subtract)

        def scale_xa(g, j):
            nc.scalar.activation(out=xa_rows[g][:, j, :], in_=kept[g][j][:], func=ACT.Copy, scale=fa_sb[g][:, j : j + 1])

        def scale_xa_vector(g, j):
            nc.vector.tensor_scalar(out=xa_rows[g][:, j, :], in0=kept[g][j][:], scalar1=fa_sb[g][:, j : j + 1],
                                    scalar2=None, op0=ALU.mult)

        def scale_xc(g, j):
            nc.scalar.activation(out=xc_rows[g][:, j, :], in_=cut[g][j][:], func=ACT.Copy, scale=fb_sb[g][:, j : j + 1])

        def scale_xc_vector(g, j):
            nc.vector.tensor_scalar(out=xc_rows[g][:, j, :], in0=cut[g][j][:], scalar1=fb_sb[g][:, j : j + 1],
                                    scalar2=None, op0=ALU.mult)

        def pack(copy, packed, rows, t0, t1):
            copy(out=packed[:, t0:t1, :].rearrange("p (c i) j -> p c j i", i=RUN),
                 in_=rows[:, :, t0:t1].rearrange("p j (c i) -> p c j i", i=RUN))

        def quantize(packed, codes, exps, fmt, t0, t1):
            nc.vector.quantize_mx(out=codes[:, t0:t1].bitcast(fmt), scales=exps[:, t0:t1],
                                  in_=packed[:, t0:t1, :].rearrange("p t j -> p (t j)"))

        def multiply_xc(g):
            for n in range(N_TILES):
                nc.tensor.matmul_mx(out=acc[n][:], lhsT=wb[:, g, 4 * P * n : 4 * P * (n + 1)].bitcast(E4M3X4),
                                    lhsT_scale=wb_exp[:, g, P * n : P * (n + 1)],
                                    rhs=xc_codes[g][:].bitcast(E5M2X4), rhs_scale=xc_exp[g][:],
                                    start=(g == 0), stop=False)

        def multiply_xa(g, t0, t1, last):
            for n in range(N_TILES):
                nc.tensor.matmul_mx(out=acc[n][:, t0:t1], lhsT=wa[:, g, 2 * P * n : 2 * P * (n + 1)].bitcast(E2M1X4),
                                    lhsT_scale=wa_exp[:, g, P * n : P * (n + 1)],
                                    rhs=xa_codes[g][:, t0:t1].bitcast(E4M3X4), rhs_scale=xa_exp[g][:, t0:t1],
                                    start=False, stop=last)

        on_vector = nc.vector.tensor_copy
        on_scalar = nc.scalar.copy

        for half in halves:
            clamp(0, 0, half)
        scale_xa(0, 0)
        for half in halves:
            subtract(0, 0, half)
        scale_xc(0, 0)
        clamp(0, 1)
        for j in range(1, PACK - 1):
            clamp(0, j + 1)
            scale_xa(0, j)
            subtract(0, j)
            scale_xc(0, j)
        subtract(0, 3)
        scale_xc(0, 3)
        scale_xa(0, 3)
        for j in (0, 1):
            clamp(1, j)
        for j in (0, 1):
            subtract(1, j)
            scale_xc(1, j)
        clamp(1, 2)
        pack(on_vector, xc_packed[0], xc_rows[0], 0, T)
        clamp(1, 3)
        quantize(xc_packed[0], xc_codes[0], xc_exp[0], E5M2X4, 0, T)
        multiply_xc(0)
        pack(on_scalar, xa_packed[0], xa_rows[0], 0, T)
        subtract(1, 2)
        scale_xc(1, 2)
        subtract(1, 3)
        scale_xa(1, 0)
        quantize(xa_packed[0], xa_codes[0], xa_exp[0], E4M3X4, 0, T)
        multiply_xa(0, 0, T, False)
        scale_xc_vector(1, 3)
        scale_xa_vector(1, 3)
        scale_xa(1, 1)
        scale_xa(1, 2)
        for t0 in (0, T // 2):
            pack(on_vector, xc_packed[1], xc_rows[1], t0, t0 + T // 2)
        for t0 in (0, T // 2):
            quantize(xc_packed[1], xc_codes[1], xc_exp[1], E5M2X4, t0, t0 + T // 2)
        multiply_xc(1)
        pack(on_scalar, xa_packed[1], xa_rows[1], T // 2, T)
        pack(on_scalar, xa_packed[1], xa_rows[1], SPLIT, T // 2)
        pack(on_vector, xa_packed[1], xa_rows[1], 0, SPLIT)
        for t0 in (T // 2, 0):
            quantize(xa_packed[1], xa_codes[1], xa_exp[1], E4M3X4, t0, t0 + T // 2)
        multiply_xa(1, 0, T, True)
        for n in range(N_TILES):
            copy = on_scalar if n % 2 == 0 else on_vector
            for cols in (halves if n == 0 else [slice(0, T)]):
                copy(out=result[n][:, cols], in_=acc[n][:, cols])
                nc.sync.dma_start(out=out[P * n : P * (n + 1), cols], in_=result[n][:, cols])
